import numpy as np
import ml_dtypes


def mxq(x, axis, fmt="e4m3"):
    dtype, down = {"e4m3": (ml_dtypes.float8_e4m3fn, 7), "e5m2": (ml_dtypes.float8_e5m2, 14)}[fmt]
    v = np.moveaxis(np.asarray(x, np.float32).astype(ml_dtypes.bfloat16).astype(np.float64), axis, -1)
    blocks = v.reshape(v.shape[:-1] + (-1, 32))
    amax = np.abs(blocks).max(-1, keepdims=True)
    byte = np.maximum(np.where(amax > 0, np.frexp(amax)[1] - 1 + 127, 0) - down, 1)
    scale = np.exp2(byte - 127.0)
    codes = (blocks / scale).astype(np.float32).astype(dtype).astype(np.float64)
    return np.moveaxis((codes * scale).reshape(v.shape), -1, axis)


WIDE = False


def mx_kscale(k, group=512):
    if not WIDE:
        return np.ones(k)
    levels = np.array([18, -18])
    if group != 512:
        return np.exp2(np.random.permutation(np.resize(levels, k // group))).repeat(group)
    if k % 512:
        return np.exp2(np.random.permutation(np.resize(levels, k // 32))).repeat(32)
    a = np.empty((k // 512, 16))
    for p in range(k // 512):
        a[p, :8] = np.random.permutation(np.resize(levels, 8))
        for g in range(8):
            far = levels[np.abs(levels - a[p, g]) >= 10]
            a[p, g + 8] = far[np.random.randint(len(far))]
    return np.exp2(a.ravel()).repeat(32)


def f64(x):
    return np.asarray(x).astype(np.float64)


def silu(v):
    return v / (1.0 + np.exp(-v))


G, D, M, N = 8, 128, 128, 512


def setup_inputs():
    n = np.random.standard_normal
    s = mx_kscale(D, 0)[:, None]
    return {
        "x": (n((G, D, N)) * s).astype(np.float32),
        "w": (n((G, D, M)) / np.sqrt(D) / s).astype(np.float32),
        "u": (n((G, D, M)) / np.sqrt(D) / s).astype(np.float32),
        "b": (0.5 * n((G, M, 1))).astype(np.float32),
    }


def reference(x, w, u, b):
    xq = mxq(f64(x), 1, "e4m3")
    h = mxq(f64(w), 1, "e4m3").transpose(0, 2, 1) @ xq
    g = mxq(f64(u), 1, "e4m3").transpose(0, 2, 1) @ xq
    h = h + f64(b)
    y = silu(h) * g
    return y

@@ -1,0 +1,130 @@
+from contextlib import ExitStack
+
+import concourse.mybir as mybir
+
+G, D, M, N = 8, 128, 128, 512
+FLOPS = 2 * 2 * G * D * M * N
+
+F32 = mybir.dt.float32
+BF16 = mybir.dt.bfloat16
+U32 = mybir.dt.uint32
+U8 = mybir.dt.uint8
+FP8X4 = mybir.dt.float8_e4m3fn_x4
+SILU = mybir.ActivationFunctionType.Silu
+MULT = mybir.AluOpType.mult
+ADD = mybir.AluOpType.add
+
+P = 128
+PACK = 4
+ROWS = D // PACK
+SIDE = P // ROWS
+NMM = 128
+CHUNKS = [[0,0,256],[0,256,256],[1,0,256],[1,256,256]]
+LOADS = ["w0","x0","u0","x1","w1","x2","u1","x3"]
+ORDER = [["il","V","w0",0,128],["q","w0"],["bt"],["il","V","x0",0,160],["il","S","x0",160,256],["q","x0"],["mm","w",0,[0,1,2,3],0,256],["il","S","u0",0,128],["q","u0"],["mm","u",0,[0,1,2,3],0,256],["silu",0,0,0,256],["silu",0,1,0,256],["silu",0,2,0,256],["silu",0,3,0,256],["il","V","x1",0,256],["mul",0,0,0,256],["q","x1"],["mul",0,1,0,256],["mul",0,2,0,256],["mul",0,3,0,256],["st",0,0,4,0,256],["mm","w",0,[0],256,512],["mm","w",0,[1],256,512],["mm","u",0,[0],256,512],["mm","w",0,[2],256,512],["mm","u",0,[1],256,512],["mm","w",0,[3],256,512],["mm","u",0,[2],256,512],["mm","u",0,[3],256,512],["il","S","w1",0,128],["silu",0,0,256,512],["silu",0,1,256,512],["silu",0,2,256,512],["silu",0,3,256,512],["il","V","x2",0,256],["q","w1"],["q","x2"],["mul",0,0,256,512],["mul",0,1,256,512],["mul",0,2,256,512],["mul",0,3,256,512],["st",0,0,4,256,512],["il","S","u1",0,128],["q","u1"],["mm","w",1,[0],0,256],["mm","w",1,[1],0,256],["mm","u",1,[0],0,256],["mm","w",1,[2],0,256],["mm","u",1,[1],0,256],["mm","w",1,[3],0,256],["mm","u",1,[2],0,256],["mm","u",1,[3],0,256],["il","S","x3",160,256],["il","V","x3",0,160],["silu",1,0,0,256],["silu",1,1,0,256],["silu",1,2,0,256],["silu",1,3,0,256],["mul",1,0,0,256],["q","x3"],["mul",1,1,0,256],["mul",1,2,0,256],["mul",1,3,0,256],["st",1,0,4,0,256],["mm","w",1,[0],256,512],["mm","w",1,[1],256,512],["mm","u",1,[0],256,512],["mm","w",1,[2],256,512],["mm","u",1,[1],256,512],["mm","w",1,[3],256,512],["mm","u",1,[2],256,512],["mm","u",1,[3],256,512],["silu",1,0,256,512],["silu",1,1,256,512],["silu",1,2,256,512],["silu",1,3,256,512],["mul",1,0,256,512],["mul",1,1,256,512],["st",1,0,2,256,512],["mul",1,2,256,512],["mul",1,3,256,512],["st",1,2,4,256,512]]
+
+
+def tile_rows_gglu_silu_bias_kernel(tc, x, w, u, b, out):
+    nc = tc.nc
+    with ExitStack() as ctx:
+        sb = ctx.enter_context(tc.tile_pool(name="sb", bufs=1))
+        ps = ctx.enter_context(tc.psum_pool(name="ps", bufs=1))
+        ctx.enter_context(tc.manual_schedule())
+
+        src = {}
+        for s in range(2):
+            gs = slice(SIDE * s, SIDE * (s + 1))
+            src["w%d" % s] = w[gs].rearrange("g (p j) m -> (g p) j m", j=PACK)
+            src["u%d" % s] = u[gs].rearrange("g (p j) m -> (g p) j m", j=PACK)
+        for k, (s, n0, wd) in enumerate(CHUNKS):
+            gs = slice(SIDE * s, SIDE * (s + 1))
+            src["x%d" % k] = x[gs].rearrange("g (p j) n -> (g p) j n", j=PACK)[:, :, n0 : n0 + wd]
+
+        raw, grp, codes, scales = {}, {}, {}, {}
+        for name, ap in src.items():
+            wd = ap.shape[2]
+            raw[name] = sb.tile([P, PACK, wd], F32, name="raw_" + name, align_bytes=64)
+            grp[name] = sb.tile([P, wd, PACK], BF16, name="grp_" + name, align_bytes=64)
+        for s in range(2):
+            for t in "wux":
+                wd = N if t == "x" else M
+                codes[t, s] = sb.tile([P, wd], U32, name="codes_%s%d" % (t, s), align_bytes=64)
+                scales[t, s] = sb.tile([P, wd], U8, name="scales_%s%d" % (t, s), align_bytes=64)
+        hb = [ps.tile([M, N], F32, name="h%d" % c) for c in range(SIDE)]
+        gb = [ps.tile([M, N], F32, name="g%d" % c) for c in range(SIDE)]
+        act = [sb.tile([M, SIDE, N], F32, name="act%d" % s) for s in range(2)]
+        res = [sb.tile([M, SIDE, N], F32, name="res%d" % s) for s in range(2)]
+        brow = sb.tile([P, 32], F32, name="brow", align_bytes=64)
+        bcol = sb.tile([P, 32], F32, name="bcol", align_bytes=64)
+        warm = sb.tile([P, 8], F32, name="warm")
+        warm2 = sb.tile([P, 8], F32, name="warm2")
+
+        nc.vector.memset(brow[:], 0.0)
+        nc.scalar.dma_start(out=brow[0:P:4, :], in_=b.rearrange("g (q i) o -> q g (i o)", i=32))
+        nc.vector.memset(warm[:], 0.0)
+        nc.scalar.activation(out=warm2[:, 0:1], in_=warm[:, 0:1], func=SILU)
+
+        for name in LOADS:
+            nc.sync.dma_start(out=raw[name][:], in_=src[name])
+
+        def il(eng, name, a, z):
+            o = grp[name][:, a:z, :].rearrange("p (c i) t -> p c t i", i=4)
+            i = raw[name][:, :, a:z].rearrange("p t (c i) -> p c t i", i=4)
+            if eng == "V":
+                nc.vector.tensor_copy(out=o, in_=i)
+            elif eng == "S":
+                nc.scalar.copy(out=o, in_=i)
+            else:
+                nc.gpsimd.tensor_scalar(out=o, in0=i, scalar1=1.0, scalar2=0.0, op0=MULT, op1=ADD)
+
+        def quant(name):
+            if name[0] == "x":
+                s, n0, wd = CHUNKS[int(name[1:])]
+            else:
+                s, n0, wd = int(name[1:]), 0, M
+            nc.vector.quantize_mx(
+                out=codes[name[0], s][:, n0 : n0 + wd].bitcast(FP8X4),
+                scales=scales[name[0], s][:, n0 : n0 + wd],
+                in_=grp[name][:].rearrange("p n t -> p (n t)"),
+            )
+
+        def mm(t, s, c, n0):
+            rows = slice(ROWS * c, ROWS * (c + 1))
+            cols = slice(n0, n0 + NMM)
+            nc.tensor.matmul_mx(
+                out=(hb if t == "w" else gb)[c][:, cols],
+                lhsT=codes[t, s][rows, :].bitcast(FP8X4),
+                lhsT_scale=scales[t, s][rows, :],
+                rhs=codes["x", s][rows, cols].bitcast(FP8X4),
+                rhs_scale=scales["x", s][rows, cols],
+                start=True,
+                stop=True,
+            )
+
+        for op in ORDER:
+            kind = op[0]
+            if kind == "il":
+                il(op[1], op[2], op[3], op[4])
+            elif kind == "q":
+                quant(op[1])
+            elif kind == "bt":
+                nc.vector.transpose(out=bcol[:], in_=brow[:])
+            elif kind == "mm":
+                t, s, cs, a, z = op[1:]
+                for n0 in range(a, z, NMM):
+                    for c in cs:
+                        mm(t, s, c, n0)
+            elif kind == "silu":
+                s, c, a, z = op[1:]
+                g = SIDE * s + c
+                nc.scalar.activation(out=act[s][:, c, a:z], in_=hb[c][:, a:z], func=SILU, bias=bcol[:, 4 * g : 4 * g + 1])
+            elif kind == "mul":
+                s, c, a, z = op[1:]
+                nc.vector.tensor_tensor(out=res[s][:, c, a:z], in0=gb[c][:, a:z], in1=act[s][:, c, a:z], op=MULT)
+            elif kind == "st":
+                s, c0, c1, a, z = op[1:6]
+                eng = nc.scalar if len(op) > 6 else nc.sync
+                eng.dma_start(
+                    out=out[SIDE * s + c0 : SIDE * s + c1, :, a:z].rearrange("g m n -> m g n"),
+                    in_=res[s][:, c0:c1, a:z],
+                )

@@ -18,10 +18,10 @@ P = 128
 PACK = 4
 ROWS = D // PACK
 SIDE = P // ROWS
-NMM = 128
+NMM = 512
 CHUNKS = [[0,0,256],[0,256,256],[1,0,256],[1,256,256]]
-LOADS = ["w0","x0","u0","x1","w1","x2","u1","x3"]
-ORDER = [["il","V","w0",0,128],["q","w0"],["bt"],["il","V","x0",0,160],["il","S","x0",160,256],["q","x0"],["mm","w",0,[0,1,2,3],0,256],["il","S","u0",0,128],["q","u0"],["mm","u",0,[0,1,2,3],0,256],["silu",0,0,0,256],["silu",0,1,0,256],["silu",0,2,0,256],["silu",0,3,0,256],["il","V","x1",0,256],["mul",0,0,0,256],["q","x1"],["mul",0,1,0,256],["mul",0,2,0,256],["mul",0,3,0,256],["st",0,0,4,0,256],["mm","w",0,[0],256,512],["mm","w",0,[1],256,512],["mm","u",0,[0],256,512],["mm","w",0,[2],256,512],["mm","u",0,[1],256,512],["mm","w",0,[3],256,512],["mm","u",0,[2],256,512],["mm","u",0,[3],256,512],["il","S","w1",0,128],["silu",0,0,256,512],["silu",0,1,256,512],["silu",0,2,256,512],["silu",0,3,256,512],["il","V","x2",0,256],["q","w1"],["q","x2"],["mul",0,0,256,512],["mul",0,1,256,512],["mul",0,2,256,512],["mul",0,3,256,512],["st",0,0,4,256,512],["il","S","u1",0,128],["q","u1"],["mm","w",1,[0],0,256],["mm","w",1,[1],0,256],["mm","u",1,[0],0,256],["mm","w",1,[2],0,256],["mm","u",1,[1],0,256],["mm","w",1,[3],0,256],["mm","u",1,[2],0,256],["mm","u",1,[3],0,256],["il","S","x3",160,256],["il","V","x3",0,160],["silu",1,0,0,256],["silu",1,1,0,256],["silu",1,2,0,256],["silu",1,3,0,256],["mul",1,0,0,256],["q","x3"],["mul",1,1,0,256],["mul",1,2,0,256],["mul",1,3,0,256],["st",1,0,4,0,256],["mm","w",1,[0],256,512],["mm","w",1,[1],256,512],["mm","u",1,[0],256,512],["mm","w",1,[2],256,512],["mm","u",1,[1],256,512],["mm","w",1,[3],256,512],["mm","u",1,[2],256,512],["mm","u",1,[3],256,512],["silu",1,0,256,512],["silu",1,1,256,512],["silu",1,2,256,512],["silu",1,3,256,512],["mul",1,0,256,512],["mul",1,1,256,512],["st",1,0,2,256,512],["mul",1,2,256,512],["mul",1,3,256,512],["st",1,2,4,256,512]]
+LOADS = ["x0","x1","w0","u0","w1","x2","x3","u1"]
+ORDER = [["bt"],["il","V","x0",0,256],["q","x0"],["il","V","x1",0,160],["il","S","x1",160,256],["il","S","w0",80,128],["q","x1"],["il","V","w0",0,80],["q","w0"],["mm","w",0,[0,1,2,3],0,512],["il","S","u0",0,128],["il","V","w1",0,128],["q","u0"],["mm","u",0,[0,1,2,3],0,512],["q","w1"],["silu",0,0,0,512],["silu",0,1,0,512],["silu",0,2,0,512],["silu",0,3,0,512],["il","V","x2",0,256],["mul",0,0,0,512],["st",0,0,1,0,512],["q","x2"],["il","V","x3",0,176],["il","S","x3",176,256],["q","x3"],["mm","w",1,[0,1,2,3],0,512],["il","S","u1",0,128],["mul",0,1,0,512],["st",0,1,2,0,512],["q","u1"],["mm","u",1,[0,1],0,512],["mul",0,2,0,512],["st",0,2,3,0,512],["mm","u",1,[2],0,512],["mul",0,3,0,512],["st",0,3,4,0,512],["mm","u",1,[3],0,512],["silu",1,0,0,512],["silu",1,1,0,512],["silu",1,2,0,512],["silu",1,3,0,512],["mul",1,0,0,512],["st",1,0,1,0,512],["mul",1,1,0,512],["st",1,1,2,0,512],["mul",1,2,0,512],["st",1,2,3,0,512],["mul",1,3,0,512],["st",1,3,4,0,512]]
 
 
 def tile_rows_gglu_silu_bias_kernel(tc, x, w, u, b, out):

@@ -11,120 +11,206 @@ U32 = mybir.dt.uint32
 U8 = mybir.dt.uint8
 FP8X4 = mybir.dt.float8_e4m3fn_x4
 SILU = mybir.ActivationFunctionType.Silu
-MULT = mybir.AluOpType.mult
-ADD = mybir.AluOpType.add
 
 P = 128
 PACK = 4
 ROWS = D // PACK
 SIDE = P // ROWS
-NMM = 512
-CHUNKS = [[0,0,256],[0,256,256],[1,0,256],[1,256,256]]
-LOADS = ["x0","x1","w0","u0","w1","x2","x3","u1"]
-ORDER = [["bt"],["il","V","x0",0,256],["q","x0"],["il","V","x1",0,160],["il","S","x1",160,256],["il","S","w0",80,128],["q","x1"],["il","V","w0",0,80],["q","w0"],["mm","w",0,[0,1,2,3],0,512],["il","S","u0",0,128],["il","V","w1",0,128],["q","u0"],["mm","u",0,[0,1,2,3],0,512],["q","w1"],["silu",0,0,0,512],["silu",0,1,0,512],["silu",0,2,0,512],["silu",0,3,0,512],["il","V","x2",0,256],["mul",0,0,0,512],["st",0,0,1,0,512],["q","x2"],["il","V","x3",0,176],["il","S","x3",176,256],["q","x3"],["mm","w",1,[0,1,2,3],0,512],["il","S","u1",0,128],["mul",0,1,0,512],["st",0,1,2,0,512],["q","u1"],["mm","u",1,[0,1],0,512],["mul",0,2,0,512],["st",0,2,3,0,512],["mm","u",1,[2],0,512],["mul",0,3,0,512],["st",0,3,4,0,512],["mm","u",1,[3],0,512],["silu",1,0,0,512],["silu",1,1,0,512],["silu",1,2,0,512],["silu",1,3,0,512],["mul",1,0,0,512],["st",1,0,1,0,512],["mul",1,1,0,512],["st",1,1,2,0,512],["mul",1,2,0,512],["st",1,2,3,0,512],["mul",1,3,0,512],["st",1,3,4,0,512]]
+BANK = 512
+CHUNK = 256
+PASS = 128
+BLOCK = 32
+BIAS_STEP = BLOCK // G
+
+VECTOR_SHARE_FIRST_WEIGHTS = 80
+VECTOR_SHARE_SECOND_HALF = 64
+VECTOR_SHARE_LAST_CHUNK = 144
+
+HEAT_BEFORE_CHUNK_0 = 23
+HEAT_BEFORE_CHUNK_1 = 11
+HEAT_BEFORE_CHUNK_2 = 12
 
 
 def tile_rows_gglu_silu_bias_kernel(tc, x, w, u, b, out):
     nc = tc.nc
     with ExitStack() as ctx:
-        sb = ctx.enter_context(tc.tile_pool(name="sb", bufs=1))
-        ps = ctx.enter_context(tc.psum_pool(name="ps", bufs=1))
+        sbuf = ctx.enter_context(tc.tile_pool(name="sbuf", bufs=1))
+        psum = ctx.enter_context(tc.psum_pool(name="psum", bufs=1))
         ctx.enter_context(tc.manual_schedule())
 
-        src = {}
-        for s in range(2):
-            gs = slice(SIDE * s, SIDE * (s + 1))
-            src["w%d" % s] = w[gs].rearrange("g (p j) m -> (g p) j m", j=PACK)
-            src["u%d" % s] = u[gs].rearrange("g (p j) m -> (g p) j m", j=PACK)
-        for k, (s, n0, wd) in enumerate(CHUNKS):
-            gs = slice(SIDE * s, SIDE * (s + 1))
-            src["x%d" % k] = x[gs].rearrange("g (p j) n -> (g p) j n", j=PACK)[:, :, n0 : n0 + wd]
+        def load(name, tensor, s, first, width):
+            rows = tensor[SIDE * s : SIDE * (s + 1)].rearrange("g (p j) n -> (g p) j n", j=PACK)
+            raw = sbuf.tile([P, PACK, width], F32, name="raw_" + name, align_bytes=64)
+            nc.sync.dma_start(out=raw[:], in_=rows[:, :, first : first + width])
+            return raw
 
-        raw, grp, codes, scales = {}, {}, {}, {}
-        for name, ap in src.items():
-            wd = ap.shape[2]
-            raw[name] = sb.tile([P, PACK, wd], F32, name="raw_" + name, align_bytes=64)
-            grp[name] = sb.tile([P, wd, PACK], BF16, name="grp_" + name, align_bytes=64)
-        for s in range(2):
-            for t in "wux":
-                wd = N if t == "x" else M
-                codes[t, s] = sb.tile([P, wd], U32, name="codes_%s%d" % (t, s), align_bytes=64)
-                scales[t, s] = sb.tile([P, wd], U8, name="scales_%s%d" % (t, s), align_bytes=64)
-        hb = [ps.tile([M, N], F32, name="h%d" % c) for c in range(SIDE)]
-        gb = [ps.tile([M, N], F32, name="g%d" % c) for c in range(SIDE)]
-        act = [sb.tile([M, SIDE, N], F32, name="act%d" % s) for s in range(2)]
-        res = [sb.tile([M, SIDE, N], F32, name="res%d" % s) for s in range(2)]
-        brow = sb.tile([P, 32], F32, name="brow", align_bytes=64)
-        bcol = sb.tile([P, 32], F32, name="bcol", align_bytes=64)
-        warm = sb.tile([P, 8], F32, name="warm")
-        warm2 = sb.tile([P, 8], F32, name="warm2")
+        def operand(name, width):
+            values = sbuf.tile([P, width, PACK], BF16, name="values_" + name, align_bytes=64)
+            codes = sbuf.tile([P, width], U32, name="codes_" + name, align_bytes=64)
+            scales = sbuf.tile([P, width], U8, name="scales_" + name, align_bytes=64)
+            return values, codes, scales
 
-        nc.vector.memset(brow[:], 0.0)
-        nc.scalar.dma_start(out=brow[0:P:4, :], in_=b.rearrange("g (q i) o -> q g (i o)", i=32))
-        nc.vector.memset(warm[:], 0.0)
-        nc.scalar.activation(out=warm2[:, 0:1], in_=warm[:, 0:1], func=SILU)
-
-        for name in LOADS:
-            nc.sync.dma_start(out=raw[name][:], in_=src[name])
-
-        def il(eng, name, a, z):
-            o = grp[name][:, a:z, :].rearrange("p (c i) t -> p c t i", i=4)
-            i = raw[name][:, :, a:z].rearrange("p t (c i) -> p c t i", i=4)
-            if eng == "V":
-                nc.vector.tensor_copy(out=o, in_=i)
-            elif eng == "S":
-                nc.scalar.copy(out=o, in_=i)
-            else:
-                nc.gpsimd.tensor_scalar(out=o, in0=i, scalar1=1.0, scalar2=0.0, op0=MULT, op1=ADD)
-
-        def quant(name):
-            if name[0] == "x":
-                s, n0, wd = CHUNKS[int(name[1:])]
-            else:
-                s, n0, wd = int(name[1:]), 0, M
-            nc.vector.quantize_mx(
-                out=codes[name[0], s][:, n0 : n0 + wd].bitcast(FP8X4),
-                scales=scales[name[0], s][:, n0 : n0 + wd],
-                in_=grp[name][:].rearrange("p n t -> p (n t)"),
+        def interleave(copy, op, at, raw, first, last):
+            copy(
+                out=op[0][:, at + first : at + last, :].rearrange("p (c i) j -> p c j i", i=2),
+                in_=raw[:, :, first:last].rearrange("p j (c i) -> p c j i", i=2),
             )
 
-        def mm(t, s, c, n0):
-            rows = slice(ROWS * c, ROWS * (c + 1))
-            cols = slice(n0, n0 + NMM)
+        def interleave_shared(op, at, raw, vector_share):
+            interleave(nc.vector.tensor_copy, op, at, raw, 0, vector_share)
+            interleave(nc.scalar.copy, op, at, raw, vector_share, raw.shape[2])
+
+        def quantize(op, first, last):
+            values, codes, scales = op
+            nc.vector.quantize_mx(
+                out=codes[:, first:last].bitcast(FP8X4),
+                scales=scales[:, first:last],
+                in_=values[:, first:last, :].rearrange("p c j -> p (c j)"),
+            )
+
+        def mx_pass(sums, rows, stationary, at, moving, first):
             nc.tensor.matmul_mx(
-                out=(hb if t == "w" else gb)[c][:, cols],
-                lhsT=codes[t, s][rows, :].bitcast(FP8X4),
-                lhsT_scale=scales[t, s][rows, :],
-                rhs=codes["x", s][rows, cols].bitcast(FP8X4),
-                rhs_scale=scales["x", s][rows, cols],
+                out=sums,
+                lhsT=stationary[1][rows, at : at + M].bitcast(FP8X4),
+                lhsT_scale=stationary[2][rows, at : at + M],
+                rhs=moving[1][rows, first : first + PASS].bitcast(FP8X4),
+                rhs_scale=moving[2][rows, first : first + PASS],
                 start=True,
                 stop=True,
             )
 
-        for op in ORDER:
-            kind = op[0]
-            if kind == "il":
-                il(op[1], op[2], op[3], op[4])
-            elif kind == "q":
-                quant(op[1])
-            elif kind == "bt":
-                nc.vector.transpose(out=bcol[:], in_=brow[:])
-            elif kind == "mm":
-                t, s, cs, a, z = op[1:]
-                for n0 in range(a, z, NMM):
-                    for c in cs:
-                        mm(t, s, c, n0)
-            elif kind == "silu":
-                s, c, a, z = op[1:]
-                g = SIDE * s + c
-                nc.scalar.activation(out=act[s][:, c, a:z], in_=hb[c][:, a:z], func=SILU, bias=bcol[:, 4 * g : 4 * g + 1])
-            elif kind == "mul":
-                s, c, a, z = op[1:]
-                nc.vector.tensor_tensor(out=res[s][:, c, a:z], in0=gb[c][:, a:z], in1=act[s][:, c, a:z], op=MULT)
-            elif kind == "st":
-                s, c0, c1, a, z = op[1:6]
-                eng = nc.scalar if len(op) > 6 else nc.sync
-                eng.dma_start(
-                    out=out[SIDE * s + c0 : SIDE * s + c1, :, a:z].rearrange("g m n -> m g n"),
-                    in_=res[s][:, c0:c1, a:z],
-                )
+        weights = [operand("weights%d" % s, 2 * M) for s in range(2)]
+        chunks = [operand("x%d" % k, CHUNK) for k in range(4)]
+        gates = [sbuf.tile([M, SIDE, CHUNK], F32, name="gate%d" % k) for k in range(4)]
+        results = [sbuf.tile([M, SIDE, CHUNK], F32, name="result%d" % k) for k in range(4)]
+
+        banks = [psum.tile([M, BANK], F32, name="bank%d" % i) for i in range(8)]
+        w_sums = [banks[c][:, 0:CHUNK] for c in range(SIDE)]
+        u_sums = [banks[SIDE + c][:, 0:CHUNK] for c in range(SIDE - 1)] + [banks[SIDE - 1][:, CHUNK:BANK]]
+        heat_sums = banks[7][:, 0:PASS]
+
+        bias_rows = sbuf.tile([P, BLOCK], F32, name="bias_rows", align_bytes=64)
+        bias = sbuf.tile([P, BLOCK], F32, name="bias", align_bytes=64)
+        nc.gpsimd.memset(bias_rows[:], 0.0)
+        nc.scalar.dma_start(
+            out=bias_rows[0:P:BIAS_STEP, :], in_=b.rearrange("g (q i) o -> q g (i o)", i=BLOCK)
+        )
+
+        table_in = sbuf.tile([P, 1], F32, name="table_in")
+        table_out = sbuf.tile([P, 1], F32, name="table_out")
+        nc.gpsimd.memset(table_in[:], 0.0)
+        nc.scalar.activation(out=table_out[:], in_=table_in[:], func=SILU)
+
+        ones = operand("ones", PASS)
+        nc.vector.memset(ones[0][:], 1.0)
+        quantize(ones, 0, PASS)
+
+        def heat(count):
+            for i in range(count):
+                mx_pass(heat_sums, slice(0, P), ones, 0, ones, 0)
+
+        x0_low = load("x0_low", x, 0, 0, PASS)
+        w0 = load("w0", w, 0, 0, M)
+        x0_high = load("x0_high", x, 0, PASS, PASS)
+        u0 = load("u0", u, 0, 0, M)
+        x1 = load("x1", x, 0, CHUNK, CHUNK)
+        w1 = load("w1", w, 1, 0, M)
+        x2 = load("x2", x, 1, 0, CHUNK)
+        u1 = load("u1", u, 1, 0, M)
+        x3 = load("x3", x, 1, CHUNK, CHUNK)
+
+        def product(sums, at, k, c, first):
+            rows = slice(ROWS * c, ROWS * (c + 1))
+            mx_pass(sums[c][:, first : first + PASS], rows, weights[k // 2], at, chunks[k], first)
+
+        def products(k, c):
+            for sums, at in ((w_sums, 0), (u_sums, M)):
+                for first in range(0, CHUNK, PASS):
+                    product(sums, at, k, c, first)
+
+        def silu(k, c):
+            column = BIAS_STEP * (SIDE * (k // 2) + c)
+            nc.scalar.activation(
+                out=gates[k][:, c, :], in_=w_sums[c], func=SILU, bias=bias[:, column : column + 1]
+            )
+
+        def multiply(k, c):
+            nc.vector.tensor_tensor(
+                out=results[k][:, c, :], in0=u_sums[c], in1=gates[k][:, c, :], op=mybir.AluOpType.mult
+            )
+
+        def store(k, first_tile, last_tile):
+            groups = slice(SIDE * (k // 2) + first_tile, SIDE * (k // 2) + last_tile)
+            columns = slice(CHUNK * (k % 2), CHUNK * (k % 2 + 1))
+            nc.sync.dma_start(
+                out=out[groups, :, columns].rearrange("g m n -> m g n"),
+                in_=results[k][:, first_tile:last_tile, :],
+            )
+
+        heat(HEAT_BEFORE_CHUNK_0)
+        nc.vector.transpose(out=bias[:], in_=bias_rows[:])
+        interleave(nc.vector.tensor_copy, chunks[0], 0, x0_low, 0, PASS)
+        interleave_shared(weights[0], 0, w0, VECTOR_SHARE_FIRST_WEIGHTS)
+        quantize(chunks[0], 0, PASS)
+        quantize(weights[0], 0, M)
+        for c in range(SIDE):
+            product(w_sums, 0, 0, c, 0)
+        interleave_shared(chunks[0], PASS, x0_high, VECTOR_SHARE_SECOND_HALF)
+        quantize(chunks[0], PASS, CHUNK)
+        for c in range(SIDE):
+            product(w_sums, 0, 0, c, PASS)
+        interleave_shared(weights[0], M, u0, VECTOR_SHARE_FIRST_WEIGHTS)
+        quantize(weights[0], M, 2 * M)
+        for first in range(0, CHUNK, PASS):
+            for c in range(SIDE):
+                product(u_sums, M, 0, c, first)
+        heat(HEAT_BEFORE_CHUNK_1)
+
+        for c in range(SIDE):
+            silu(0, c)
+        interleave(nc.scalar.copy, weights[1], 0, w1, 0, M)
+        interleave(nc.vector.tensor_copy, chunks[1], 0, x1, 0, CHUNK)
+        multiply(0, 0)
+        quantize(chunks[1], 0, CHUNK)
+        products(1, 0)
+        multiply(0, 1)
+        store(0, 0, 2)
+        products(1, 1)
+        multiply(0, 2)
+        products(1, 2)
+        multiply(0, 3)
+        store(0, 2, 4)
+        products(1, 3)
+        heat(HEAT_BEFORE_CHUNK_2)
+
+        silu(1, 0)
+        silu(1, 1)
+        interleave(nc.scalar.copy, weights[1], M, u1, 0, M)
+        silu(1, 2)
+        silu(1, 3)
+        interleave(nc.vector.tensor_copy, chunks[2], 0, x2, 0, CHUNK)
+        multiply(1, 0)
+        quantize(chunks[2], 0, CHUNK)
+        multiply(1, 1)
+        store(1, 0, 2)
+        quantize(weights[1], 0, 2 * M)
+        products(2, 0)
+        products(2, 1)
+        multiply(1, 2)
+        products(2, 2)
+        interleave_shared(chunks[3], 0, x3, VECTOR_SHARE_LAST_CHUNK)
+        multiply(1, 3)
+        store(1, 2, 4)
+        products(2, 3)
+        quantize(chunks[3], 0, CHUNK)
+
+        for c in range(SIDE):
+            silu(2, c)
+            multiply(2, c)
+            store(2, c, c + 1)
+            products(3, c)
+
+        for c in range(SIDE):
+            silu(3, c)
+            multiply(3, c)
+            store(3, c, c + 1)

from contextlib import ExitStack

import concourse.mybir as mybir

G, D, M, N = 8, 128, 128, 512
FLOPS = 2 * 2 * G * D * M * N

F32 = mybir.dt.float32
BF16 = mybir.dt.bfloat16
U32 = mybir.dt.uint32
U8 = mybir.dt.uint8
FP8X4 = mybir.dt.float8_e4m3fn_x4
SILU = mybir.ActivationFunctionType.Silu

P = 128
PACK = 4
ROWS = D // PACK
SIDE = P // ROWS
BANK = 512
CHUNK = 256
PASS = 128
BLOCK = 32
BIAS_STEP = BLOCK // G

VECTOR_SHARE_FIRST_WEIGHTS = 80
VECTOR_SHARE_SECOND_HALF = 64
VECTOR_SHARE_LAST_CHUNK = 144

HEAT_BEFORE_CHUNK_0 = 23
HEAT_BEFORE_CHUNK_1 = 11
HEAT_BEFORE_CHUNK_2 = 12


def tile_rows_gglu_silu_bias_kernel(tc, x, w, u, b, out):
    nc = tc.nc
    with ExitStack() as ctx:
        sbuf = ctx.enter_context(tc.tile_pool(name="sbuf", bufs=1))
        psum = ctx.enter_context(tc.psum_pool(name="psum", bufs=1))
        ctx.enter_context(tc.manual_schedule())

        def load(name, tensor, s, first, width):
            rows = tensor[SIDE * s : SIDE * (s + 1)].rearrange("g (p j) n -> (g p) j n", j=PACK)
            raw = sbuf.tile([P, PACK, width], F32, name="raw_" + name, align_bytes=64)
            nc.sync.dma_start(out=raw[:], in_=rows[:, :, first : first + width])
            return raw

        def operand(name, width):
            values = sbuf.tile([P, width, PACK], BF16, name="values_" + name, align_bytes=64)
            codes = sbuf.tile([P, width], U32, name="codes_" + name, align_bytes=64)
            scales = sbuf.tile([P, width], U8, name="scales_" + name, align_bytes=64)
            return values, codes, scales

        def interleave(copy, op, at, raw, first, last):
            copy(
                out=op[0][:, at + first : at + last, :].rearrange("p (c i) j -> p c j i", i=2),
                in_=raw[:, :, first:last].rearrange("p j (c i) -> p c j i", i=2),
            )

        def interleave_shared(op, at, raw, vector_share):
            interleave(nc.vector.tensor_copy, op, at, raw, 0, vector_share)
            interleave(nc.scalar.copy, op, at, raw, vector_share, raw.shape[2])

        def quantize(op, first, last):
            values, codes, scales = op
            nc.vector.quantize_mx(
                out=codes[:, first:last].bitcast(FP8X4),
                scales=scales[:, first:last],
                in_=values[:, first:last, :].rearrange("p c j -> p (c j)"),
            )

        def mx_pass(sums, rows, stationary, at, moving, first):
            nc.tensor.matmul_mx(
                out=sums,
                lhsT=stationary[1][rows, at : at + M].bitcast(FP8X4),
                lhsT_scale=stationary[2][rows, at : at + M],
                rhs=moving[1][rows, first : first + PASS].bitcast(FP8X4),
                rhs_scale=moving[2][rows, first : first + PASS],
                start=True,
                stop=True,
            )

        weights = [operand("weights%d" % s, 2 * M) for s in range(2)]
        chunks = [operand("x%d" % k, CHUNK) for k in range(4)]
        gates = [sbuf.tile([M, SIDE, CHUNK], F32, name="gate%d" % k) for k in range(4)]
        results = [sbuf.tile([M, SIDE, CHUNK], F32, name="result%d" % k) for k in range(4)]

        banks = [psum.tile([M, BANK], F32, name="bank%d" % i) for i in range(8)]
        w_sums = [banks[c][:, 0:CHUNK] for c in range(SIDE)]
        u_sums = [banks[SIDE + c][:, 0:CHUNK] for c in range(SIDE - 1)] + [banks[SIDE - 1][:, CHUNK:BANK]]
        heat_sums = banks[7][:, 0:PASS]

        bias_rows = sbuf.tile([P, BLOCK], F32, name="bias_rows", align_bytes=64)
        bias = sbuf.tile([P, BLOCK], F32, name="bias", align_bytes=64)
        nc.gpsimd.memset(bias_rows[:], 0.0)
        nc.scalar.dma_start(
            out=bias_rows[0:P:BIAS_STEP, :], in_=b.rearrange("g (q i) o -> q g (i o)", i=BLOCK)
        )

        table_in = sbuf.tile([P, 1], F32, name="table_in")
        table_out = sbuf.tile([P, 1], F32, name="table_out")
        nc.gpsimd.memset(table_in[:], 0.0)
        nc.scalar.activation(out=table_out[:], in_=table_in[:], func=SILU)

        ones = operand("ones", PASS)
        nc.vector.memset(ones[0][:], 1.0)
        quantize(ones, 0, PASS)

        def heat(count):
            for i in range(count):
                mx_pass(heat_sums, slice(0, P), ones, 0, ones, 0)

        x0_low = load("x0_low", x, 0, 0, PASS)
        w0 = load("w0", w, 0, 0, M)
        x0_high = load("x0_high", x, 0, PASS, PASS)
        u0 = load("u0", u, 0, 0, M)
        x1 = load("x1", x, 0, CHUNK, CHUNK)
        w1 = load("w1", w, 1, 0, M)
        x2 = load("x2", x, 1, 0, CHUNK)
        u1 = load("u1", u, 1, 0, M)
        x3 = load("x3", x, 1, CHUNK, CHUNK)

        def product(sums, at, k, c, first):
            rows = slice(ROWS * c, ROWS * (c + 1))
            mx_pass(sums[c][:, first : first + PASS], rows, weights[k // 2], at, chunks[k], first)

        def products(k, c):
            for sums, at in ((w_sums, 0), (u_sums, M)):
                for first in range(0, CHUNK, PASS):
                    product(sums, at, k, c, first)

        def silu(k, c):
            column = BIAS_STEP * (SIDE * (k // 2) + c)
            nc.scalar.activation(
                out=gates[k][:, c, :], in_=w_sums[c], func=SILU, bias=bias[:, column : column + 1]
            )

        def multiply(k, c):
            nc.vector.tensor_tensor(
                out=results[k][:, c, :], in0=u_sums[c], in1=gates[k][:, c, :], op=mybir.AluOpType.mult
            )

        def store(k, first_tile, last_tile):
            groups = slice(SIDE * (k // 2) + first_tile, SIDE * (k // 2) + last_tile)
            columns = slice(CHUNK * (k % 2), CHUNK * (k % 2 + 1))
            nc.sync.dma_start(
                out=out[groups, :, columns].rearrange("g m n -> m g n"),
                in_=results[k][:, first_tile:last_tile, :],
            )

        heat(HEAT_BEFORE_CHUNK_0)
        nc.vector.transpose(out=bias[:], in_=bias_rows[:])
        interleave(nc.vector.tensor_copy, chunks[0], 0, x0_low, 0, PASS)
        interleave_shared(weights[0], 0, w0, VECTOR_SHARE_FIRST_WEIGHTS)
        quantize(chunks[0], 0, PASS)
        quantize(weights[0], 0, M)
        for c in range(SIDE):
            product(w_sums, 0, 0, c, 0)
        interleave_shared(chunks[0], PASS, x0_high, VECTOR_SHARE_SECOND_HALF)
        quantize(chunks[0], PASS, CHUNK)
        for c in range(SIDE):
            product(w_sums, 0, 0, c, PASS)
        interleave_shared(weights[0], M, u0, VECTOR_SHARE_FIRST_WEIGHTS)
        quantize(weights[0], M, 2 * M)
        for first in range(0, CHUNK, PASS):
            for c in range(SIDE):
                product(u_sums, M, 0, c, first)
        heat(HEAT_BEFORE_CHUNK_1)

        for c in range(SIDE):
            silu(0, c)
        interleave(nc.scalar.copy, weights[1], 0, w1, 0, M)
        interleave(nc.vector.tensor_copy, chunks[1], 0, x1, 0, CHUNK)
        multiply(0, 0)
        quantize(chunks[1], 0, CHUNK)
        products(1, 0)
        multiply(0, 1)
        store(0, 0, 2)
        products(1, 1)
        multiply(0, 2)
        products(1, 2)
        multiply(0, 3)
        store(0, 2, 4)
        products(1, 3)
        heat(HEAT_BEFORE_CHUNK_2)

        silu(1, 0)
        silu(1, 1)
        interleave(nc.scalar.copy, weights[1], M, u1, 0, M)
        silu(1, 2)
        silu(1, 3)
        interleave(nc.vector.tensor_copy, chunks[2], 0, x2, 0, CHUNK)
        multiply(1, 0)
        quantize(chunks[2], 0, CHUNK)
        multiply(1, 1)
        store(1, 0, 2)
        quantize(weights[1], 0, 2 * M)
        products(2, 0)
        products(2, 1)
        multiply(1, 2)
        products(2, 2)
        interleave_shared(chunks[3], 0, x3, VECTOR_SHARE_LAST_CHUNK)
        multiply(1, 3)
        store(1, 2, 4)
        products(2, 3)
        quantize(chunks[3], 0, CHUNK)

        for c in range(SIDE):
            silu(2, c)
            multiply(2, c)
            store(2, c, c + 1)
            products(3, c)

        for c in range(SIDE):
            silu(3, c)
            multiply(3, c)
            store(3, c, c + 1)
